import numpy as np
import ml_dtypes


def mxq(x, axis, fmt="e4m3"):
    dtype, down = {"e4m3": (ml_dtypes.float8_e4m3fn, 7), "e5m2": (ml_dtypes.float8_e5m2, 14)}[fmt]
    v = np.moveaxis(np.asarray(x, np.float32).astype(ml_dtypes.bfloat16).astype(np.float64), axis, -1)
    blocks = v.reshape(v.shape[:-1] + (-1, 32))
    amax = np.abs(blocks).max(-1, keepdims=True)
    byte = np.maximum(np.where(amax > 0, np.frexp(amax)[1] - 1 + 127, 0) - down, 1)
    scale = np.exp2(byte - 127.0)
    codes = (blocks / scale).astype(np.float32).astype(dtype).astype(np.float64)
    return np.moveaxis((codes * scale).reshape(v.shape), -1, axis)


WIDE = False


def mx_kscale(k):
    if not WIDE:
        return np.ones(k)
    levels = np.array([10, -10, 5, -5, 0])
    if k % 512:
        return np.exp2(np.random.permutation(np.resize(levels, k // 32))).repeat(32)
    a = np.empty((k // 512, 16))
    for p in range(k // 512):
        a[p, :8] = np.random.permutation(np.resize(levels, 8))
        for g in range(8):
            far = levels[np.abs(levels - a[p, g]) >= 10]
            a[p, g + 8] = far[np.random.randint(len(far))]
    return np.exp2(a.ravel()).repeat(32)


BF16 = ml_dtypes.bfloat16


def bf(x):
    return np.asarray(x, np.float32).astype(BF16)


def f64(x):
    return np.asarray(x).astype(np.float64)

def planes(Y):
    n, m = Y.shape
    b = f64(bf(Y)).reshape(n // 32, 32, m)
    amax = np.abs(b).max(1)
    byte = np.clip(np.where(amax > 0, np.frexp(amax)[1] - 1 + 127 - 7, 1), 1, 254)
    codes = (b * np.exp2(127.0 - byte)[:, None, :]).reshape(n, m).astype(np.float32).astype(ml_dtypes.float8_e4m3fn).view(np.uint8)
    words = codes.reshape(n // 512, 128, 4, m).transpose(0, 1, 3, 2)
    return np.ascontiguousarray(words), np.ascontiguousarray(byte.astype(np.uint8).reshape(n // 512, 16, m))


N, D, K = 2048, 1024, 512


def sigmoid(v):
    return 1.0 / (1.0 + np.exp(-v))


def threshold_logits(xgq, w, s, b):
    return (xgq @ mxq(f64(w), 0, "e4m3")) * f64(s)[None, :] + f64(b)[None, :]


def ordinal_labels(y, t):
    return np.where(f64(y)[:, None] > f64(t)[None, :], 1.0, 0.0)


def setup_inputs():
    u, v = mx_kscale(D), mx_kscale(K)
    return {"x": bf(np.random.standard_normal((N, D))),
            "g": bf((1.0 + 0.1 * np.random.standard_normal(D)) * u),
            "w": bf(np.random.standard_normal((D, K)) / np.sqrt(D) / u[:, None] / v[None, :]),
            "s": bf((1.0 + 0.1 * np.random.standard_normal(K)) * v),
            "b": bf(0.5 * np.random.standard_normal(K)),
            "y": bf(np.random.standard_normal(N)),
            "t": bf(np.random.standard_normal(K))}


def core(x, g, w, s, b, y, t):
    xgq = mxq(f64(x) * f64(g)[None, :], 1, "e4m3")
    z = threshold_logits(xgq, w, s, b)
    l = ordinal_labels(y, t)
    d = (sigmoid(z) - l) * f64(s)[None, :]
    return f64(g)[None, :] * (mxq(d, 1, "e4m3") @ mxq(f64(w).T, 0, "e4m3"))


def reference(x, g, w, s, b, y, t):
    R_out = core(x, g, w, s, b, y, t)
    words, scales = planes(R_out)
    return R_out, words, scales

@@ -1,0 +1,371 @@
+from contextlib import ExitStack
+
+import concourse.mybir as mybir
+from concourse.masks import make_identity
+
+N, D, K = 2048, 1024, 512
+FLOPS = 4 * N * D * K
+
+F32 = mybir.dt.float32
+BF16 = mybir.dt.bfloat16
+U32 = mybir.dt.uint32
+I32 = mybir.dt.int32
+U8 = mybir.dt.uint8
+FP8X4 = mybir.dt.float8_e4m3fn_x4
+ALU = mybir.AluOpType
+ACT = mybir.ActivationFunctionType
+
+P = 128
+CH = 512
+NCH = N // CH
+NH = D // 512
+
+
+def tile_ordinaldepththresholdfeaturegradient_x1_kernel(tc, x, g, w, s, b, y, t, out_0, out_1, out_2):
+    nc = tc.nc
+    with ExitStack() as ctx:
+        keep = ctx.enter_context(tc.tile_pool(name="keep", bufs=1))
+        xin = ctx.enter_context(tc.tile_pool(name="xin", bufs=NCH))
+        work = ctx.enter_context(tc.tile_pool(name="work", bufs=2))
+        outs = ctx.enter_context(tc.tile_pool(name="outs", bufs=4))
+        psum = ctx.enter_context(tc.psum_pool(name="psum", bufs=2))
+        psum_o = ctx.enter_context(tc.psum_pool(name="psum_o", bufs=4))
+        ctx.enter_context(tc.manual_schedule())
+
+        w_raw = keep.tile([P, NH, 4, K], BF16, align_bytes=64, name="w_raw")
+        w_v = w.rearrange("(h p j) k -> p h j k", h=NH, j=4)
+        for h in range(NH):
+            nc.sync.dma_start(out=w_raw[:, h], in_=w_v[:, h])
+        x_raw = []
+        for c in range(NCH):
+            xr = xin.tile([P, 4, D], BF16, align_bytes=64, name="xr")
+            xv = x[c * CH : (c + 1) * CH, :].rearrange("(p t) d -> p t d", t=4)
+            for tp in range(2):
+                nc.sync.dma_start(out=xr[:, 2 * tp : 2 * tp + 2, :], in_=xv[:, 2 * tp : 2 * tp + 2, :])
+            x_raw.append(xr)
+        g4 = keep.tile([P, NH, 2, 2], BF16, align_bytes=64, name="g4")
+        nc.scalar.dma_start(out=g4[:], in_=g.rearrange("(h p u e) -> p h u e", h=NH, u=2, e=2))
+        ycol = keep.tile([P, NCH, 4], BF16, align_bytes=64, name="ycol")
+        nc.scalar.dma_start(out=ycol[:], in_=y.rearrange("(c p t) -> p c t", c=NCH, t=4))
+        vecs = keep.tile([P, 3, 16], BF16, align_bytes=64, name="vecs")
+        for i, v in enumerate((t, s, b)):
+            nc.scalar.dma_start(out=vecs[:, i, 0:4], in_=v.rearrange("(p q) -> p q", q=4))
+        g8 = keep.tile([P, 8], BF16, align_bytes=64, name="g8")
+        nc.scalar.dma_start(out=g8[:], in_=g.rearrange("(p c) -> p c", c=8))
+
+        warm = keep.tile([P, 1], F32, name="warm")
+        warm2 = keep.tile([P, 1], F32, name="warm2")
+        nc.vector.memset(warm[:], 0.0)
+        nc.scalar.activation(out=warm2[:], in_=warm[:], func=ACT.Sigmoid)
+
+        id32 = keep.tile([P, P], F32, align_bytes=64, name="id32")
+        make_identity(nc, id32[:])
+        id16 = keep.tile([P, P], BF16, align_bytes=64, name="id16")
+        nc.vector.tensor_copy(out=id16[:], in_=id32[:])
+        vec32 = keep.tile([P, 3, 4], F32, align_bytes=64, name="vec32")
+        nc.vector.tensor_copy(out=vec32[:], in_=vecs[:, :, 0:4])
+
+        y_bc = keep.tile([P, N], BF16, align_bytes=64, name="y_bc")
+        for hf in range(2):
+            yp = psum_o.tile([P, N // 2], BF16, name="o_ps")
+            for i in range(8):
+                j = hf * 8 + i
+                nc.tensor.transpose(
+                    yp[:, i * P : (i + 1) * P],
+                    ycol[:].rearrange("p c t -> p (c t)")[:, j : j + 1].to_broadcast([P, P]),
+                    id16[:],
+                )
+            nc.scalar.copy(out=y_bc[:, hf * N // 2 : (hf + 1) * N // 2], in_=yp[:])
+
+        w_gr = keep.tile([P, NH, K, 4], BF16, align_bytes=64, name="w_gr")
+        w_codes = keep.tile([P, NH, K], U32, align_bytes=64, name="w_codes")
+        w_scales = keep.tile([P, NH, K], U8, align_bytes=64, name="w_scales")
+
+        def w_inter(h, eng):
+            dst = w_gr[:, h].rearrange("p (q m) j -> p q m j", q=4)
+            srcv = w_raw[:, h].rearrange("p j (m q) -> p q m j", q=4)
+            for q in range(4):
+                if eng == 0:
+                    nc.scalar.copy(out=dst[:, q], in_=srcv[:, q])
+                else:
+                    nc.vector.tensor_copy(out=dst[:, q], in_=srcv[:, q])
+
+        def w_quant(h):
+            nc.vector.quantize_mx(
+                out=w_codes[:, h].bitcast(FP8X4),
+                scales=w_scales[:, h],
+                in_=w_gr[:, h].rearrange("p k j -> p (k j)"),
+            )
+
+        xs = {}
+
+        def x_alloc(c):
+            xs[c] = (
+                work.tile([P, NH, CH, 4], BF16, align_bytes=64, name="x_gr"),
+                work.tile([P, NH, CH], U32, align_bytes=64, name="x_codes"),
+                work.tile([P, NH, CH], U8, align_bytes=64, name="x_scales"),
+            )
+
+        def x_mul(c, tp):
+            words = x_raw[c][:].bitcast(F32)
+            for h in range(NH):
+                xt = psum.tile([P, 2, 256], F32, name="xt")
+                for tt in range(2):
+                    for u in range(2):
+                        nc.tensor.transpose(
+                            xt[:, u, tt * P : (tt + 1) * P],
+                            words[:, 2 * tp + tt, 256 * h + u : 256 * (h + 1) : 2],
+                            id32[:],
+                        )
+                nc.vector.tensor_tensor(
+                    out=xs[c][0][:, h, 256 * tp : 256 * (tp + 1), :].rearrange("p n (u e) -> p n u e", u=2),
+                    in0=xt[:].bitcast(BF16).rearrange("p u (n e) -> p n u e", e=2),
+                    in1=g4[:, h].unsqueeze(1).to_broadcast([P, 256, 2, 2]),
+                    op=ALU.mult,
+                )
+
+        def x_quant(c, h):
+            gr, codes, scales = xs[c]
+            nc.vector.quantize_mx(
+                out=codes[:, h].bitcast(FP8X4), scales=scales[:, h], in_=gr[:, h].rearrange("p n j -> p (n j)")
+            )
+
+        wt_gr = keep.tile([P, D, 4], BF16, align_bytes=64, name="wt_gr")
+        wt_codes = keep.tile([P, D], U32, align_bytes=64, name="wt_codes")
+        wt_scales = keep.tile([P, D], U8, align_bytes=64, name="wt_scales")
+
+        def wt_turn():
+            words = w_raw[:].bitcast(F32)
+            dst = wt_gr[:].rearrange("p d e -> p (d e)").bitcast(F32).rearrange("p (h m j u) -> p h m j u", h=NH, j=4, u=2)
+            for h in range(NH):
+                for jp in range(2):
+                    wt = psum_o.tile([P, 2, 2, P], F32, name="o_ps")
+                    for jj in range(2):
+                        for u in range(2):
+                            nc.tensor.transpose(wt[:, jj, u, :], words[:, h, 2 * jp + jj, u : 256 : 2], id32[:])
+                    nc.scalar.copy(
+                        out=dst[:, h, :, 2 * jp : 2 * jp + 2, :], in_=wt[:].rearrange("p j u m -> p m j u")
+                    )
+
+        def wt_quant():
+            nc.vector.quantize_mx(
+                out=wt_codes[:].bitcast(FP8X4), scales=wt_scales[:], in_=wt_gr[:].rearrange("p d j -> p (d j)")
+            )
+
+        g_bc = keep.tile([P, D], BF16, align_bytes=64, name="g_bc")
+
+        def g_spread():
+            gp = psum_o.tile([P, 4, P], F32, name="o_ps")
+            gw = g8[:].bitcast(F32)
+            for i in range(4):
+                nc.tensor.transpose(gp[:, i, :], gw[:, i : i + 1].to_broadcast([P, P]), id32[:])
+            nc.scalar.copy(
+                out=g_bc[:].bitcast(F32).rearrange("p (m i) -> p m i", i=4), in_=gp[:].rearrange("p i m -> p m i")
+            )
+
+        ls = keep.tile([P, 4, N], BF16, align_bytes=64, name="ls")
+
+        def labels(q):
+            nc.vector.tensor_scalar(
+                out=ls[:, q, :],
+                in0=y_bc[:],
+                scalar1=vec32[:, 0, q : q + 1],
+                scalar2=vec32[:, 1, q : q + 1],
+                op0=ALU.is_gt,
+                op1=ALU.mult,
+            )
+
+        ds = {}
+
+        def d_alloc(c):
+            ds[c] = dict(
+                sig=work.tile([P, 4, CH], F32, align_bytes=64, name="sig"),
+                d=work.tile([P, 4, CH], F32, align_bytes=64, name="d32"),
+                gr=work.tile([P, CH, 4], BF16, align_bytes=64, name="d_gr"),
+                codes=work.tile([P, CH], U32, align_bytes=64, name="d_codes"),
+                scales=work.tile([P, CH], U8, align_bytes=64, name="d_scales"),
+            )
+
+        def mm1(c, q):
+            z = psum.tile([P, CH], F32, name="z")
+            for h in range(NH):
+                nc.tensor.matmul_mx(
+                    out=z[:],
+                    lhsT=w_codes[:, h, q * P : (q + 1) * P].bitcast(FP8X4),
+                    lhsT_scale=w_scales[:, h, q * P : (q + 1) * P],
+                    rhs=xs[c][1][:, h].bitcast(FP8X4),
+                    rhs_scale=xs[c][2][:, h],
+                    start=(h == 0),
+                    stop=(h == NH - 1),
+                )
+            nc.scalar.activation(
+                out=ds[c]["sig"][:, q, :],
+                in_=z[:],
+                func=ACT.Sigmoid,
+                bias=vec32[:, 2, q : q + 1],
+                scale=vec32[:, 1, q : q + 1],
+            )
+
+        def d_sub(c, q):
+            nc.vector.scalar_tensor_tensor(
+                out=ds[c]["d"][:, q, :],
+                in0=ds[c]["sig"][:, q, :],
+                scalar=vec32[:, 1, q : q + 1],
+                in1=ls[:, q, c * CH : (c + 1) * CH],
+                op0=ALU.mult,
+                op1=ALU.subtract,
+            )
+
+        def inter(dst, srct, lo, hi, on_vector):
+            o = dst[:, lo:hi, :].rearrange("p (c i) q -> p c q i", i=4)
+            i_ = srct[:, :, lo:hi].rearrange("p q (c i) -> p c q i", i=4)
+            if on_vector:
+                nc.vector.tensor_copy(out=o, in_=i_)
+            else:
+                nc.scalar.copy(out=o, in_=i_)
+
+        def d_quant(c):
+            e = ds[c]
+            nc.vector.quantize_mx(
+                out=e["codes"][:].bitcast(FP8X4), scales=e["scales"][:], in_=e["gr"][:].rearrange("p n j -> p (n j)")
+            )
+
+        os_ = {}
+
+        def o_alloc(c, dh):
+            os_[(c, dh)] = dict(
+                o=outs.tile([P, 4, 512], F32, align_bytes=64, name="o32"),
+                gr=work.tile([P, 512, 4], BF16, align_bytes=64, name="o_gr"),
+                codes=outs.tile([P, 512], U32, align_bytes=64, name="o_codes"),
+            )
+            if dh == 0:
+                os_[c] = work.tile([P, D], U8, align_bytes=64, name="o_scales")
+
+        def mm2(c, dh, tt):
+            o = psum_o.tile([P, 512], F32, name="o_ps")
+            nc.tensor.matmul_mx(
+                out=o[:],
+                lhsT=ds[c]["codes"][:, tt * P : (tt + 1) * P].bitcast(FP8X4),
+                lhsT_scale=ds[c]["scales"][:, tt * P : (tt + 1) * P],
+                rhs=wt_codes[:, dh * 512 : (dh + 1) * 512].bitcast(FP8X4),
+                rhs_scale=wt_scales[:, dh * 512 : (dh + 1) * 512],
+                start=True,
+                stop=True,
+            )
+            return o
+
+        def o_mul(c, dh, tt, o):
+            nc.vector.tensor_tensor(
+                out=os_[(c, dh)]["o"][:, tt, :], in0=o[:], in1=g_bc[:, dh * 512 : (dh + 1) * 512], op=ALU.mult
+            )
+
+        def o_store(c, dh, t0, t1):
+            nc.sync.dma_start(
+                out=out_0[c * CH : (c + 1) * CH, dh * 512 : (dh + 1) * 512].rearrange("(p t) d -> p t d", t=4)[:, t0:t1, :],
+                in_=os_[(c, dh)]["o"][:, t0:t1, :],
+            )
+
+        def o_quant(c, dh):
+            e = os_[(c, dh)]
+            nc.vector.quantize_mx(
+                out=e["codes"][:].bitcast(FP8X4),
+                scales=os_[c][:, dh * 512 : (dh + 1) * 512],
+                in_=e["gr"][:].rearrange("p d j -> p (d j)"),
+            )
+            nc.sync.dma_start(
+                out=out_1[c, :, dh * 512 : (dh + 1) * 512, :].rearrange("p m t -> p (m t)").bitcast(I32),
+                in_=e["codes"][:].bitcast(I32),
+            )
+            if dh == 1:
+                for qd in range(4):
+                    nc.sync.dma_start(
+                        out=out_2[c, 4 * qd : 4 * qd + 4, :].bitcast(I32),
+                        in_=os_[c][32 * qd : 32 * qd + 4, :].bitcast(I32),
+                    )
+
+        w_inter(0, 0)
+        w_inter(1, 1)
+        x_alloc(0)
+        x_mul(0, 0)
+        w_quant(0)
+        x_mul(0, 1)
+        w_quant(1)
+        x_quant(0, 0)
+        x_quant(0, 1)
+        wt_turn()
+        for q in range(4):
+            labels(q)
+        d_alloc(0)
+        for q in range(4):
+            mm1(0, q)
+        x_alloc(1)
+        x_mul(1, 0)
+        g_spread()
+
+        for c in range(NCH):
+            last = c == NCH - 1
+            for q in range(4):
+                d_sub(c, q)
+            if c == 0:
+                inter(ds[c]["gr"], ds[c]["d"], 0, CH, False)
+                x_mul(1, 1)
+                x_quant(1, 0)
+                x_quant(1, 1)
+                wt_quant()
+                d_quant(c)
+                x_alloc(2)
+                x_mul(2, 0)
+            elif c == 1:
+                o_quant(0, 0)
+                inter(os_[(0, 1)]["gr"], os_[(0, 1)]["o"], 0, 512, False)
+                inter(ds[c]["gr"], ds[c]["d"], 0, CH, False)
+                x_mul(2, 1)
+                x_quant(2, 0)
+                x_quant(2, 1)
+                x_alloc(3)
+                x_mul(3, 0)
+                d_quant(c)
+                o_quant(0, 1)
+            else:
+                if c == 2:
+                    inter(ds[c]["gr"], ds[c]["d"], 0, 256, True)
+                    inter(ds[c]["gr"], ds[c]["d"], 256, CH, False)
+                    o_quant(c - 1, 0)
+                    inter(os_[(c - 1, 1)]["gr"], os_[(c - 1, 1)]["o"], 0, 512, False)
+                    d_quant(c)
+                    x_mul(3, 1)
+                    x_quant(3, 0)
+                    x_quant(3, 1)
+                else:
+                    inter(ds[c]["gr"], ds[c]["d"], 0, 256, True)
+                    inter(ds[c]["gr"], ds[c]["d"], 256, CH, False)
+                    o_quant(c - 1, 0)
+                    inter(os_[(c - 1, 1)]["gr"], os_[(c - 1, 1)]["o"], 0, 512, False)
+                    d_quant(c)
+            banks = [None] * 4
+            o_alloc(c, 0)
+            for tt in range(4):
+                banks[tt] = mm2(c, 0, tt)
+            if not last:
+                d_alloc(c + 1)
+            o_alloc(c, 1)
+            for tt in range(4):
+                o_mul(c, 0, tt, banks[tt])
+                if not last:
+                    mm1(c + 1, tt)
+                banks[tt] = mm2(c, 1, tt)
+            o_store(c, 0, 0, 4)
+            inter(os_[(c, 0)]["gr"], os_[(c, 0)]["o"], 0, 512, False)
+            for tt in range(4):
+                o_mul(c, 1, tt, banks[tt])
+                if last:
+                    o_store(c, 1, tt, tt + 1)
+            if c >= 2:
+                o_quant(c - 1, 1)
+            if not last:
+                o_store(c, 1, 0, 4)
+            else:
+                inter(os_[(c, 1)]["gr"], os_[(c, 1)]["o"], 0, 192, False)
+                inter(os_[(c, 1)]["gr"], os_[(c, 1)]["o"], 192, 512, True)
+                o_quant(c, 0)
+                o_quant(c, 1)

@@ -34,10 +34,11 @@ def tile_ordinaldepththresholdfeaturegradient_x1_kernel(tc, x, g, w, s, b, y, t,
 
         w_raw = keep.tile([P, NH, 4, K], BF16, align_bytes=64, name="w_raw")
         w_v = w.rearrange("(h p j) k -> p h j k", h=NH, j=4)
-        for h in range(NH):
-            nc.sync.dma_start(out=w_raw[:, h], in_=w_v[:, h])
         x_raw = []
         for c in range(NCH):
+            if c == 1:
+                for h in range(NH):
+                    nc.sync.dma_start(out=w_raw[:, h], in_=w_v[:, h])
             xr = xin.tile([P, 4, D], BF16, align_bytes=64, name="xr")
             xv = x[c * CH : (c + 1) * CH, :].rearrange("(p t) d -> p t d", t=4)
             for tp in range(2):
@@ -66,16 +67,17 @@ def tile_ordinaldepththresholdfeaturegradient_x1_kernel(tc, x, g, w, s, b, y, t,
         nc.vector.tensor_copy(out=vec32[:], in_=vecs[:, :, 0:4])
 
         y_bc = keep.tile([P, N], BF16, align_bytes=64, name="y_bc")
-        for hf in range(2):
-            yp = psum_o.tile([P, N // 2], BF16, name="o_ps")
-            for i in range(8):
-                j = hf * 8 + i
-                nc.tensor.transpose(
-                    yp[:, i * P : (i + 1) * P],
-                    ycol[:].rearrange("p c t -> p (c t)")[:, j : j + 1].to_broadcast([P, P]),
-                    id16[:],
-                )
-            nc.scalar.copy(out=y_bc[:, hf * N // 2 : (hf + 1) * N // 2], in_=yp[:])
+        def y_spread():
+            for hf in range(2):
+                yp = psum_o.tile([P, N // 2], BF16, name="o_ps")
+                for i in range(8):
+                    j = hf * 8 + i
+                    nc.tensor.transpose(
+                        yp[:, i * P : (i + 1) * P],
+                        ycol[:].rearrange("p c t -> p (c t)")[:, j : j + 1].to_broadcast([P, P]),
+                        id16[:],
+                    )
+                nc.scalar.copy(out=y_bc[:, hf * N // 2 : (hf + 1) * N // 2], in_=yp[:])
 
         w_gr = keep.tile([P, NH, K, 4], BF16, align_bytes=64, name="w_gr")
         w_codes = keep.tile([P, NH, K], U32, align_bytes=64, name="w_codes")
@@ -134,18 +136,16 @@ def tile_ordinaldepththresholdfeaturegradient_x1_kernel(tc, x, g, w, s, b, y, t,
         wt_codes = keep.tile([P, D], U32, align_bytes=64, name="wt_codes")
         wt_scales = keep.tile([P, D], U8, align_bytes=64, name="wt_scales")
 
-        def wt_turn():
+        def wt_turn(blocks):
             words = w_raw[:].bitcast(F32)
             dst = wt_gr[:].rearrange("p d e -> p (d e)").bitcast(F32).rearrange("p (h m j u) -> p h m j u", h=NH, j=4, u=2)
-            for h in range(NH):
-                for jp in range(2):
-                    wt = psum_o.tile([P, 2, 2, P], F32, name="o_ps")
-                    for jj in range(2):
-                        for u in range(2):
-                            nc.tensor.transpose(wt[:, jj, u, :], words[:, h, 2 * jp + jj, u : 256 : 2], id32[:])
-                    nc.scalar.copy(
-                        out=dst[:, h, :, 2 * jp : 2 * jp + 2, :], in_=wt[:].rearrange("p j u m -> p m j u")
-                    )
+            for blk in blocks:
+                h, jp = blk // 2, blk % 2
+                wt = psum_o.tile([P, 2, 2, P], F32, name="o_ps")
+                for jj in range(2):
+                    for u in range(2):
+                        nc.tensor.transpose(wt[:, jj, u, :], words[:, h, 2 * jp + jj, u : 256 : 2], id32[:])
+                nc.scalar.copy(out=dst[:, h, :, 2 * jp : 2 * jp + 2, :], in_=wt[:].rearrange("p j u m -> p m j u"))
 
         def wt_quant():
             nc.vector.quantize_mx(
@@ -230,142 +230,154 @@ def tile_ordinaldepththresholdfeaturegradient_x1_kernel(tc, x, g, w, s, b, y, t,
                 out=e["codes"][:].bitcast(FP8X4), scales=e["scales"][:], in_=e["gr"][:].rearrange("p n j -> p (n j)")
             )
 
-        os_ = {}
+        outp = {}
 
         def o_alloc(c, dh):
-            os_[(c, dh)] = dict(
+            outp[(c, dh)] = dict(
                 o=outs.tile([P, 4, 512], F32, align_bytes=64, name="o32"),
                 gr=work.tile([P, 512, 4], BF16, align_bytes=64, name="o_gr"),
                 codes=outs.tile([P, 512], U32, align_bytes=64, name="o_codes"),
             )
             if dh == 0:
-                os_[c] = work.tile([P, D], U8, align_bytes=64, name="o_scales")
+                outp[c] = work.tile([P, D], U8, align_bytes=64, name="o_scales")
 
-        def mm2(c, dh, tt):
-            o = psum_o.tile([P, 512], F32, name="o_ps")
+        def mm2(c, dh, tt, lo=0, hi=512):
+            o = psum_o.tile([P, hi - lo], F32, name="o_ps")
             nc.tensor.matmul_mx(
                 out=o[:],
                 lhsT=ds[c]["codes"][:, tt * P : (tt + 1) * P].bitcast(FP8X4),
                 lhsT_scale=ds[c]["scales"][:, tt * P : (tt + 1) * P],
-                rhs=wt_codes[:, dh * 512 : (dh + 1) * 512].bitcast(FP8X4),
-                rhs_scale=wt_scales[:, dh * 512 : (dh + 1) * 512],
+                rhs=wt_codes[:, dh * 512 + lo : dh * 512 + hi].bitcast(FP8X4),
+                rhs_scale=wt_scales[:, dh * 512 + lo : dh * 512 + hi],
                 start=True,
                 stop=True,
             )
             return o
 
-        def o_mul(c, dh, tt, o):
+        def o_mul(c, dh, tt, o, lo=0, hi=512):
             nc.vector.tensor_tensor(
-                out=os_[(c, dh)]["o"][:, tt, :], in0=o[:], in1=g_bc[:, dh * 512 : (dh + 1) * 512], op=ALU.mult
+                out=outp[(c, dh)]["o"][:, tt, lo:hi], in0=o[:], in1=g_bc[:, dh * 512 + lo : dh * 512 + hi], op=ALU.mult
             )
 
-        def o_store(c, dh, t0, t1):
+        def o_store(c, dh, t0, t1, lo=0, hi=512):
             nc.sync.dma_start(
-                out=out_0[c * CH : (c + 1) * CH, dh * 512 : (dh + 1) * 512].rearrange("(p t) d -> p t d", t=4)[:, t0:t1, :],
-                in_=os_[(c, dh)]["o"][:, t0:t1, :],
+                out=out_0[c * CH : (c + 1) * CH, dh * 512 + lo : dh * 512 + hi].rearrange("(p t) d -> p t d", t=4)[:, t0:t1, :],
+                in_=outp[(c, dh)]["o"][:, t0:t1, lo:hi],
             )
 
-        def o_quant(c, dh):
-            e = os_[(c, dh)]
+        def o_quant(c, dh, lo=0, hi=512):
+            e = outp[(c, dh)]
             nc.vector.quantize_mx(
-                out=e["codes"][:].bitcast(FP8X4),
-                scales=os_[c][:, dh * 512 : (dh + 1) * 512],
-                in_=e["gr"][:].rearrange("p d j -> p (d j)"),
+                out=e["codes"][:, lo:hi].bitcast(FP8X4),
+                scales=outp[c][:, dh * 512 + lo : dh * 512 + hi],
+                in_=e["gr"][:, lo:hi, :].rearrange("p d j -> p (d j)"),
             )
             nc.sync.dma_start(
-                out=out_1[c, :, dh * 512 : (dh + 1) * 512, :].rearrange("p m t -> p (m t)").bitcast(I32),
-                in_=e["codes"][:].bitcast(I32),
+                out=out_1[c, :, dh * 512 + lo : dh * 512 + hi, :].rearrange("p m t -> p (m t)").bitcast(I32),
+                in_=e["codes"][:, lo:hi].bitcast(I32),
             )
-            if dh == 1:
-                for qd in range(4):
-                    nc.sync.dma_start(
-                        out=out_2[c, 4 * qd : 4 * qd + 4, :].bitcast(I32),
-                        in_=os_[c][32 * qd : 32 * qd + 4, :].bitcast(I32),
-                    )
 
-        w_inter(0, 0)
-        w_inter(1, 1)
+        def scale_store(c):
+            for qd in range(4):
+                nc.sync.dma_start(
+                    out=out_2[c, 4 * qd : 4 * qd + 4, :].bitcast(I32),
+                    in_=outp[c][32 * qd : 32 * qd + 4, :].bitcast(I32),
+                )
+
+        def o_inter(c, dh, lo, hi, on_vector):
+            inter(outp[(c, dh)]["gr"], outp[(c, dh)]["o"], lo, hi, on_vector)
+
+        def d_inter(c, lo, hi, on_vector):
+            inter(ds[c]["gr"], ds[c]["d"], lo, hi, on_vector)
+
+        def o_half(c, dh, after_first=None):
+            o_alloc(c, dh)
+            banks = [mm2(c, dh, tt) for tt in range(4)]
+            if after_first is not None:
+                after_first()
+            for tt in range(4):
+                o_mul(c, dh, tt, banks[tt])
+                if tt % 2 == 1:
+                    o_store(c, dh, tt - 1, tt + 1)
+
+        def stage1(c, qs):
+            if 0 in qs:
+                d_alloc(c)
+            for q in qs:
+                mm1(c, q)
+
         x_alloc(0)
         x_mul(0, 0)
-        w_quant(0)
+        y_spread()
         x_mul(0, 1)
-        w_quant(1)
+        w_inter(0, 0)
         x_quant(0, 0)
         x_quant(0, 1)
-        wt_turn()
+        w_inter(1, 0)
         for q in range(4):
             labels(q)
-        d_alloc(0)
-        for q in range(4):
-            mm1(0, q)
         x_alloc(1)
         x_mul(1, 0)
+        x_mul(1, 1)
+        wt_turn((0, 1))
+        w_quant(0)
+        w_quant(1)
+        stage1(0, (0, 1, 2, 3))
+        wt_turn((2, 3))
+        x_quant(1, 0)
+        x_quant(1, 1)
+        for q in range(4):
+            d_sub(0, q)
+        x_alloc(2)
+        x_mul(2, 0)
+        d_inter(0, 0, CH, False)
         g_spread()
-
+        wt_quant()
+        d_quant(0)
         for c in range(NCH):
-            last = c == NCH - 1
-            for q in range(4):
-                d_sub(c, q)
-            if c == 0:
-                inter(ds[c]["gr"], ds[c]["d"], 0, CH, False)
-                x_mul(1, 1)
-                x_quant(1, 0)
-                x_quant(1, 1)
-                wt_quant()
-                d_quant(c)
-                x_alloc(2)
-                x_mul(2, 0)
-            elif c == 1:
-                o_quant(0, 0)
-                inter(os_[(0, 1)]["gr"], os_[(0, 1)]["o"], 0, 512, False)
-                inter(ds[c]["gr"], ds[c]["d"], 0, CH, False)
-                x_mul(2, 1)
-                x_quant(2, 0)
-                x_quant(2, 1)
-                x_alloc(3)
-                x_mul(3, 0)
-                d_quant(c)
-                o_quant(0, 1)
-            else:
+            if c < NCH - 1:
+                o_half(c, 0, lambda: stage1(c + 1, (0, 1, 2, 3)))
+                if c > 0:
+                    o_quant(c - 1, 1)
+                    scale_store(c - 1)
+                for q in range(4):
+                    d_sub(c + 1, q)
+                o_inter(c, 0, 0, 512, False)
                 if c == 2:
-                    inter(ds[c]["gr"], ds[c]["d"], 0, 256, True)
-                    inter(ds[c]["gr"], ds[c]["d"], 256, CH, False)
-                    o_quant(c - 1, 0)
-                    inter(os_[(c - 1, 1)]["gr"], os_[(c - 1, 1)]["o"], 0, 512, False)
-                    d_quant(c)
+                    d_inter(c + 1, 0, 256, True)
+                    d_inter(c + 1, 256, CH, False)
+                else:
+                    d_inter(c + 1, 0, CH, False)
+                o_half(c, 1)
+                if c == 0:
+                    x_mul(2, 1)
+                    x_quant(2, 0)
+                    x_quant(2, 1)
+                    x_alloc(3)
+                    x_mul(3, 0)
+                if c == 1:
                     x_mul(3, 1)
                     x_quant(3, 0)
                     x_quant(3, 1)
-                else:
-                    inter(ds[c]["gr"], ds[c]["d"], 0, 256, True)
-                    inter(ds[c]["gr"], ds[c]["d"], 256, CH, False)
-                    o_quant(c - 1, 0)
-                    inter(os_[(c - 1, 1)]["gr"], os_[(c - 1, 1)]["o"], 0, 512, False)
-                    d_quant(c)
-            banks = [None] * 4
-            o_alloc(c, 0)
-            for tt in range(4):
-                banks[tt] = mm2(c, 0, tt)
-            if not last:
-                d_alloc(c + 1)
-            o_alloc(c, 1)
-            for tt in range(4):
-                o_mul(c, 0, tt, banks[tt])
-                if not last:
-                    mm1(c + 1, tt)
-                banks[tt] = mm2(c, 1, tt)
-            o_store(c, 0, 0, 4)
-            inter(os_[(c, 0)]["gr"], os_[(c, 0)]["o"], 0, 512, False)
-            for tt in range(4):
-                o_mul(c, 1, tt, banks[tt])
-                if last:
-                    o_store(c, 1, tt, tt + 1)
-            if c >= 2:
-                o_quant(c - 1, 1)
-            if not last:
-                o_store(c, 1, 0, 4)
-            else:
-                inter(os_[(c, 1)]["gr"], os_[(c, 1)]["o"], 0, 192, False)
-                inter(os_[(c, 1)]["gr"], os_[(c, 1)]["o"], 192, 512, True)
+                d_quant(c + 1)
                 o_quant(c, 0)
-                o_quant(c, 1)
+                o_inter(c, 1, 0, 512, False)
+            else:
+                o_half(c, 0)
+                o_quant(c - 1, 1)
+                scale_store(c - 1)
+                o_inter(c, 0, 0, 512, False)
+                o_alloc(c, 1)
+                for lo in (0, 256):
+                    for tt in range(4):
+                        bank = mm2(c, 1, tt, lo, lo + 256)
+                        o_mul(c, 1, tt, bank, lo, lo + 256)
+                    o_store(c, 1, 0, 4, lo, lo + 256)
+                    if lo == 0:
+                        o_inter(c, 1, 0, 256, False)
+                o_quant(c, 0)
+                o_inter(c, 1, 256, 352, False)
+                o_inter(c, 1, 352, 512, True)
+                o_quant(c, 1, 0, 256)
+                o_quant(c, 1, 256, 512)
+                scale_store(c)

@@ -44,15 +44,12 @@ def tile_ordinaldepththresholdfeaturegradient_x1_kernel(tc, x, g, w, s, b, y, t,
             for tp in range(2):
                 nc.sync.dma_start(out=xr[:, 2 * tp : 2 * tp + 2, :], in_=xv[:, 2 * tp : 2 * tp + 2, :])
             x_raw.append(xr)
-        g4 = keep.tile([P, NH, 2, 2], BF16, align_bytes=64, name="g4")
-        nc.scalar.dma_start(out=g4[:], in_=g.rearrange("(h p u e) -> p h u e", h=NH, u=2, e=2))
-        ycol = keep.tile([P, NCH, 4], BF16, align_bytes=64, name="ycol")
-        nc.scalar.dma_start(out=ycol[:], in_=y.rearrange("(c p t) -> p c t", c=NCH, t=4))
-        vecs = keep.tile([P, 3, 16], BF16, align_bytes=64, name="vecs")
+        rows = keep.tile([P, 512], BF16, align_bytes=64, name="rows")
+        nc.vector.memset(rows[:].bitcast(U32), 0)
+        nc.scalar.dma_start(out=rows[0:2, :], in_=g.rearrange("(h i) -> h i", h=2))
+        nc.scalar.dma_start(out=rows[2:6, :], in_=y.rearrange("(c i) -> c i", c=NCH))
         for i, v in enumerate((t, s, b)):
-            nc.scalar.dma_start(out=vecs[:, i, 0:4], in_=v.rearrange("(p q) -> p q", q=4))
-        g8 = keep.tile([P, 8], BF16, align_bytes=64, name="g8")
-        nc.scalar.dma_start(out=g8[:], in_=g.rearrange("(p c) -> p c", c=8))
+            nc.scalar.dma_start(out=rows[6 + i : 7 + i, :], in_=v.unsqueeze(0))
 
         warm = keep.tile([P, 1], F32, name="warm")
         warm2 = keep.tile([P, 1], F32, name="warm2")
@@ -63,18 +60,25 @@ def tile_ordinaldepththresholdfeaturegradient_x1_kernel(tc, x, g, w, s, b, y, t,
         make_identity(nc, id32[:])
         id16 = keep.tile([P, P], BF16, align_bytes=64, name="id16")
         nc.vector.tensor_copy(out=id16[:], in_=id32[:])
+        cols_ps = psum_o.tile([P, 4, P], BF16, name="o_ps")
+        for k in range(4):
+            nc.tensor.transpose(cols_ps[:, k, :], rows[:, k:512:4], id16[:])
+        cols = keep.tile([P, 16, 2, 2], BF16, align_bytes=64, name="cols")
+        nc.vector.tensor_copy(
+            out=cols[:].rearrange("p r u e -> p r (u e)"), in_=cols_ps[:, :, 0:16].rearrange("p k r -> p r k")
+        )
         vec32 = keep.tile([P, 3, 4], F32, align_bytes=64, name="vec32")
-        nc.vector.tensor_copy(out=vec32[:], in_=vecs[:, :, 0:4])
+        nc.vector.tensor_copy(out=vec32[:], in_=cols[:, 6:9].rearrange("p r u e -> p r (u e)"))
 
         y_bc = keep.tile([P, N], BF16, align_bytes=64, name="y_bc")
-        def y_spread():
-            for hf in range(2):
+        def y_spread(halves):
+            for hf in halves:
                 yp = psum_o.tile([P, N // 2], BF16, name="o_ps")
                 for i in range(8):
                     j = hf * 8 + i
                     nc.tensor.transpose(
                         yp[:, i * P : (i + 1) * P],
-                        ycol[:].rearrange("p c t -> p (c t)")[:, j : j + 1].to_broadcast([P, P]),
+                        cols[:].rearrange("p r u e -> p (r u e)")[:, 8 + j : 9 + j].to_broadcast([P, P]),
                         id16[:],
                     )
                 nc.scalar.copy(out=y_bc[:, hf * N // 2 : (hf + 1) * N // 2], in_=yp[:])
@@ -92,11 +96,11 @@ def tile_ordinaldepththresholdfeaturegradient_x1_kernel(tc, x, g, w, s, b, y, t,
                 else:
                     nc.vector.tensor_copy(out=dst[:, q], in_=srcv[:, q])
 
-        def w_quant(h):
+        def w_quant():
             nc.vector.quantize_mx(
-                out=w_codes[:, h].bitcast(FP8X4),
-                scales=w_scales[:, h],
-                in_=w_gr[:, h].rearrange("p k j -> p (k j)"),
+                out=w_codes[:].rearrange("p h k -> p (h k)").bitcast(FP8X4),
+                scales=w_scales[:].rearrange("p h k -> p (h k)"),
+                in_=w_gr[:].rearrange("p h k j -> p (h k j)"),
             )
 
         xs = {}
@@ -122,14 +126,16 @@ def tile_ordinaldepththresholdfeaturegradient_x1_kernel(tc, x, g, w, s, b, y, t,
                 nc.vector.tensor_tensor(
                     out=xs[c][0][:, h, 256 * tp : 256 * (tp + 1), :].rearrange("p n (u e) -> p n u e", u=2),
                     in0=xt[:].bitcast(BF16).rearrange("p u (n e) -> p n u e", e=2),
-                    in1=g4[:, h].unsqueeze(1).to_broadcast([P, 256, 2, 2]),
+                    in1=cols[:, h].unsqueeze(1).to_broadcast([P, 256, 2, 2]),
                     op=ALU.mult,
                 )
 
-        def x_quant(c, h):
+        def x_quant(c):
             gr, codes, scales = xs[c]
             nc.vector.quantize_mx(
-                out=codes[:, h].bitcast(FP8X4), scales=scales[:, h], in_=gr[:, h].rearrange("p n j -> p (n j)")
+                out=codes[:].rearrange("p h n -> p (h n)").bitcast(FP8X4),
+                scales=scales[:].rearrange("p h n -> p (h n)"),
+                in_=gr[:].rearrange("p h n j -> p (h n j)"),
             )
 
         wt_gr = keep.tile([P, D, 4], BF16, align_bytes=64, name="wt_gr")
@@ -156,11 +162,12 @@ def tile_ordinaldepththresholdfeaturegradient_x1_kernel(tc, x, g, w, s, b, y, t,
 
         def g_spread():
             gp = psum_o.tile([P, 4, P], F32, name="o_ps")
-            gw = g8[:].bitcast(F32)
+            gw = cols[:].rearrange("p r u e -> p (r u e)").bitcast(F32)
             for i in range(4):
                 nc.tensor.transpose(gp[:, i, :], gw[:, i : i + 1].to_broadcast([P, P]), id32[:])
             nc.scalar.copy(
-                out=g_bc[:].bitcast(F32).rearrange("p (m i) -> p m i", i=4), in_=gp[:].rearrange("p i m -> p m i")
+                out=g_bc[:].bitcast(F32).rearrange("p (h m u) -> p h m u", h=NH, u=2),
+                in_=gp[:].rearrange("p (h u) m -> p h m u", h=NH),
             )
 
         ls = keep.tile([P, 4, N], BF16, align_bytes=64, name="ls")
@@ -308,32 +315,31 @@ def tile_ordinaldepththresholdfeaturegradient_x1_kernel(tc, x, g, w, s, b, y, t,
 
         x_alloc(0)
         x_mul(0, 0)
-        y_spread()
+        y_spread((0,))
         x_mul(0, 1)
+        y_spread((1,))
         w_inter(0, 0)
-        x_quant(0, 0)
-        x_quant(0, 1)
+        x_quant(0)
         w_inter(1, 0)
         for q in range(4):
             labels(q)
         x_alloc(1)
         x_mul(1, 0)
         x_mul(1, 1)
-        wt_turn((0, 1))
-        w_quant(0)
-        w_quant(1)
-        stage1(0, (0, 1, 2, 3))
-        wt_turn((2, 3))
-        x_quant(1, 0)
-        x_quant(1, 1)
-        for q in range(4):
-            d_sub(0, q)
+        wt_turn((0, 1, 2, 3))
+        w_quant()
         x_alloc(2)
         x_mul(2, 0)
+        stage1(0, (0, 1, 2, 3))
+        x_quant(1)
+        for q in range(4):
+            d_sub(0, q)
+        x_mul(2, 1)
         d_inter(0, 0, CH, False)
         g_spread()
         wt_quant()
         d_quant(0)
+        x_quant(2)
         for c in range(NCH):
             if c < NCH - 1:
                 o_half(c, 0, lambda: stage1(c + 1, (0, 1, 2, 3)))
@@ -350,16 +356,12 @@ def tile_ordinaldepththresholdfeaturegradient_x1_kernel(tc, x, g, w, s, b, y, t,
                     d_inter(c + 1, 0, CH, False)
                 o_half(c, 1)
                 if c == 0:
-                    x_mul(2, 1)
-                    x_quant(2, 0)
-                    x_quant(2, 1)
                     x_alloc(3)
                     x_mul(3, 0)
-                if c == 1:
                     x_mul(3, 1)
-                    x_quant(3, 0)
-                    x_quant(3, 1)
                 d_quant(c + 1)
+                if c == 0:
+                    x_quant(3)
                 o_quant(c, 0)
                 o_inter(c, 1, 0, 512, False)
             else:

@@ -44,12 +44,11 @@ def tile_ordinaldepththresholdfeaturegradient_x1_kernel(tc, x, g, w, s, b, y, t,
             for tp in range(2):
                 nc.sync.dma_start(out=xr[:, 2 * tp : 2 * tp + 2, :], in_=xv[:, 2 * tp : 2 * tp + 2, :])
             x_raw.append(xr)
-        rows = keep.tile([P, 512], BF16, align_bytes=64, name="rows")
-        nc.vector.memset(rows[:].bitcast(U32), 0)
-        nc.scalar.dma_start(out=rows[0:2, :], in_=g.rearrange("(h i) -> h i", h=2))
-        nc.scalar.dma_start(out=rows[2:6, :], in_=y.rearrange("(c i) -> c i", c=NCH))
+        cols = keep.tile([P, 8, 16], BF16, align_bytes=64, name="cols")
+        nc.scalar.dma_start(out=cols[:, 0, 0:8].rearrange("p (h i) -> p h i", h=NH), in_=g.rearrange("(h p i) -> p h i", h=NH, i=4))
+        nc.scalar.dma_start(out=cols[:, 1, :].rearrange("p (c i) -> p c i", c=NCH), in_=y.rearrange("(c p i) -> p c i", c=NCH, i=4))
         for i, v in enumerate((t, s, b)):
-            nc.scalar.dma_start(out=rows[6 + i : 7 + i, :], in_=v.unsqueeze(0))
+            nc.scalar.dma_start(out=cols[:, 2 + i, 0:4], in_=v.rearrange("(p i) -> p i", i=4))
 
         warm = keep.tile([P, 1], F32, name="warm")
         warm2 = keep.tile([P, 1], F32, name="warm2")
@@ -60,15 +59,9 @@ def tile_ordinaldepththresholdfeaturegradient_x1_kernel(tc, x, g, w, s, b, y, t,
         make_identity(nc, id32[:])
         id16 = keep.tile([P, P], BF16, align_bytes=64, name="id16")
         nc.vector.tensor_copy(out=id16[:], in_=id32[:])
-        cols_ps = psum_o.tile([P, 4, P], BF16, name="o_ps")
-        for k in range(4):
-            nc.tensor.transpose(cols_ps[:, k, :], rows[:, k:512:4], id16[:])
-        cols = keep.tile([P, 16, 2, 2], BF16, align_bytes=64, name="cols")
-        nc.vector.tensor_copy(
-            out=cols[:].rearrange("p r u e -> p r (u e)"), in_=cols_ps[:, :, 0:16].rearrange("p k r -> p r k")
-        )
         vec32 = keep.tile([P, 3, 4], F32, align_bytes=64, name="vec32")
-        nc.vector.tensor_copy(out=vec32[:], in_=cols[:, 6:9].rearrange("p r u e -> p r (u e)"))
+        nc.vector.tensor_copy(out=vec32[:], in_=cols[:, 2:5, 0:4])
+        g4 = cols[:, 0, 0:8].rearrange("p (h u e) -> p h u e", h=NH, u=2)
 
         y_bc = keep.tile([P, N], BF16, align_bytes=64, name="y_bc")
         def y_spread(halves):
@@ -78,7 +71,7 @@ def tile_ordinaldepththresholdfeaturegradient_x1_kernel(tc, x, g, w, s, b, y, t,
                     j = hf * 8 + i
                     nc.tensor.transpose(
                         yp[:, i * P : (i + 1) * P],
-                        cols[:].rearrange("p r u e -> p (r u e)")[:, 8 + j : 9 + j].to_broadcast([P, P]),
+                        cols[:, 1, j : j + 1].to_broadcast([P, P]),
                         id16[:],
                     )
                 nc.scalar.copy(out=y_bc[:, hf * N // 2 : (hf + 1) * N // 2], in_=yp[:])
@@ -112,21 +105,28 @@ def tile_ordinaldepththresholdfeaturegradient_x1_kernel(tc, x, g, w, s, b, y, t,
                 work.tile([P, NH, CH], U8, align_bytes=64, name="x_scales"),
             )
 
-        def x_mul(c, tp):
+        def x_turn(c, tp):
             words = x_raw[c][:].bitcast(F32)
+            xts = []
             for h in range(NH):
                 xt = psum.tile([P, 2, 256], F32, name="xt")
                 for tt in range(2):
                     for u in range(2):
+                        cols_tt = slice(tt * P, (tt + 1) * P)
                         nc.tensor.transpose(
-                            xt[:, u, tt * P : (tt + 1) * P],
+                            xt[:, u, cols_tt],
                             words[:, 2 * tp + tt, 256 * h + u : 256 * (h + 1) : 2],
                             id32[:],
                         )
+                xts.append(xt)
+            return xts
+
+        def x_mul(c, tp, xts):
+            for h in range(NH):
                 nc.vector.tensor_tensor(
                     out=xs[c][0][:, h, 256 * tp : 256 * (tp + 1), :].rearrange("p n (u e) -> p n u e", u=2),
-                    in0=xt[:].bitcast(BF16).rearrange("p u (n e) -> p n u e", e=2),
-                    in1=cols[:, h].unsqueeze(1).to_broadcast([P, 256, 2, 2]),
+                    in0=xts[h][:].bitcast(BF16).rearrange("p u (n e) -> p n u e", e=2),
+                    in1=g4[:, h].unsqueeze(1).to_broadcast([P, 256, 2, 2]),
                     op=ALU.mult,
                 )
 
@@ -162,7 +162,7 @@ def tile_ordinaldepththresholdfeaturegradient_x1_kernel(tc, x, g, w, s, b, y, t,
 
         def g_spread():
             gp = psum_o.tile([P, 4, P], F32, name="o_ps")
-            gw = cols[:].rearrange("p r u e -> p (r u e)").bitcast(F32)
+            gw = cols[:, 0, :].bitcast(F32)
             for i in range(4):
                 nc.tensor.transpose(gp[:, i, :], gw[:, i : i + 1].to_broadcast([P, P]), id32[:])
             nc.scalar.copy(
@@ -242,7 +242,7 @@ def tile_ordinaldepththresholdfeaturegradient_x1_kernel(tc, x, g, w, s, b, y, t,
         def o_alloc(c, dh):
             outp[(c, dh)] = dict(
                 o=outs.tile([P, 4, 512], F32, align_bytes=64, name="o32"),
-                gr=work.tile([P, 512, 4], BF16, align_bytes=64, name="o_gr"),
+                gr=outs.tile([P, 512, 4], BF16, align_bytes=64, name="o_gr"),
                 codes=outs.tile([P, 512], U32, align_bytes=64, name="o_codes"),
             )
             if dh == 0:
@@ -297,89 +297,129 @@ def tile_ordinaldepththresholdfeaturegradient_x1_kernel(tc, x, g, w, s, b, y, t,
         def d_inter(c, lo, hi, on_vector):
             inter(ds[c]["gr"], ds[c]["d"], lo, hi, on_vector)
 
-        def o_half(c, dh, after_first=None):
-            o_alloc(c, dh)
-            banks = [mm2(c, dh, tt) for tt in range(4)]
-            if after_first is not None:
-                after_first()
-            for tt in range(4):
-                o_mul(c, dh, tt, banks[tt])
-                if tt % 2 == 1:
-                    o_store(c, dh, tt - 1, tt + 1)
+        d_split = [0,0,0,0]
 
-        def stage1(c, qs):
-            if 0 in qs:
-                d_alloc(c)
-            for q in qs:
-                mm1(c, q)
+        def d_turn(c):
+            if d_split[c] > 0:
+                d_inter(c, 0, d_split[c], True)
+            d_inter(c, d_split[c], CH, False)
 
         x_alloc(0)
-        x_mul(0, 0)
-        y_spread((0,))
-        x_mul(0, 1)
-        y_spread((1,))
+        x_mul(0, 0, x_turn(0, 0))
+        x_mul(0, 1, x_turn(0, 1))
         w_inter(0, 0)
-        x_quant(0)
+        y_spread((0, 1))
         w_inter(1, 0)
+        x_quant(0)
+        x_alloc(1)
+        x_mul(1, 0, x_turn(1, 0))
+        x_mul(1, 1, x_turn(1, 1))
         for q in range(4):
             labels(q)
-        x_alloc(1)
-        x_mul(1, 0)
-        x_mul(1, 1)
         wt_turn((0, 1, 2, 3))
+        xt20 = x_turn(2, 0)
         w_quant()
-        x_alloc(2)
-        x_mul(2, 0)
-        stage1(0, (0, 1, 2, 3))
+        d_alloc(0)
+        mm1(0, 0)
+        mm1(0, 1)
         x_quant(1)
-        for q in range(4):
-            d_sub(0, q)
-        x_mul(2, 1)
-        d_inter(0, 0, CH, False)
-        g_spread()
+        x_alloc(2)
+        x_mul(2, 0, xt20)
+        xt21 = x_turn(2, 1)
+        mm1(0, 2)
+        mm1(0, 3)
         wt_quant()
-        d_quant(0)
+        d_sub(0, 0)
+        d_sub(0, 1)
+        x_mul(2, 1, xt21)
+        d_alloc(1)
+        mm1(1, 0)
+        xt30 = x_turn(3, 0)
+        d_sub(0, 2)
+        d_sub(0, 3)
+        d_turn(0)
+        x_alloc(3)
+        x_mul(3, 0, xt30)
+        mm1(1, 1)
+        xt31 = x_turn(3, 1)
+        mm1(1, 2)
+        g_spread()
+        mm1(1, 3)
         x_quant(2)
+        d_sub(1, 0)
+        d_quant(0)
+        d_sub(1, 1)
+        d_sub(1, 2)
+        d_sub(1, 3)
         for c in range(NCH):
-            if c < NCH - 1:
-                o_half(c, 0, lambda: stage1(c + 1, (0, 1, 2, 3)))
+            last = c == NCH - 1
+            ahead = c + 2 < NCH
+            o_alloc(c, 0)
+            o_alloc(c, 1)
+            banks = [mm2(c, 0, tt) for tt in range(4)]
+            if not last:
+                if ahead:
+                    d_alloc(c + 2)
+                o_mul(c, 0, 0, banks[0])
+                banks.append(mm2(c, 1, 0))
+                d_turn(c + 1)
+                if ahead:
+                    mm1(c + 2, 0)
+                    mm1(c + 2, 1)
+                for tt in range(1, 4):
+                    o_mul(c, 0, tt, banks[tt])
+                    banks.append(mm2(c, 1, tt))
+                    if tt % 2 == 1:
+                        o_store(c, 0, tt - 1, tt + 1)
+                if ahead:
+                    mm1(c + 2, 2)
+                    mm1(c + 2, 3)
+                o_inter(c, 0, 0, 512, False)
+                o_mul(c, 1, 0, banks[4])
+                if c > 0:
+                    o_quant(c - 1, 0)
+                o_mul(c, 1, 1, banks[5])
+                o_store(c, 1, 0, 2)
+                if ahead:
+                    d_sub(c + 2, 0)
+                if c == 0:
+                    x_mul(3, 1, xt31)
+                o_mul(c, 1, 2, banks[6])
+                d_quant(c + 1)
+                o_mul(c, 1, 3, banks[7])
+                o_store(c, 1, 2, 4)
+                o_inter(c, 1, 0, 512, False)
+                if ahead:
+                    d_sub(c + 2, 1)
+                if c == 0:
+                    x_quant(3)
+                if ahead:
+                    d_sub(c + 2, 2)
+                    d_sub(c + 2, 3)
                 if c > 0:
                     o_quant(c - 1, 1)
                     scale_store(c - 1)
-                for q in range(4):
-                    d_sub(c + 1, q)
-                o_inter(c, 0, 0, 512, False)
-                if c == 2:
-                    d_inter(c + 1, 0, 256, True)
-                    d_inter(c + 1, 256, CH, False)
-                else:
-                    d_inter(c + 1, 0, CH, False)
-                o_half(c, 1)
-                if c == 0:
-                    x_alloc(3)
-                    x_mul(3, 0)
-                    x_mul(3, 1)
-                d_quant(c + 1)
-                if c == 0:
-                    x_quant(3)
-                o_quant(c, 0)
-                o_inter(c, 1, 0, 512, False)
             else:
-                o_half(c, 0)
+                for tt in range(4):
+                    o_mul(c, 0, tt, banks[tt])
+                    if tt % 2 == 1:
+                        o_store(c, 0, tt - 1, tt + 1)
+                    banks.append(mm2(c, 1, tt, 0, 256))
+                o_quant(c - 1, 0)
+                o_inter(c, 0, 0, 512, False)
+                for tt in range(4):
+                    o_mul(c, 1, tt, banks[4 + tt], 0, 256)
+                    banks.append(mm2(c, 1, tt, 256, 512))
+                o_store(c, 1, 0, 4, 0, 256)
                 o_quant(c - 1, 1)
                 scale_store(c - 1)
-                o_inter(c, 0, 0, 512, False)
-                o_alloc(c, 1)
-                for lo in (0, 256):
-                    for tt in range(4):
-                        bank = mm2(c, 1, tt, lo, lo + 256)
-                        o_mul(c, 1, tt, bank, lo, lo + 256)
-                    o_store(c, 1, 0, 4, lo, lo + 256)
-                    if lo == 0:
-                        o_inter(c, 1, 0, 256, False)
+                o_inter(c, 1, 0, 256, False)
+                for tt in range(4):
+                    o_mul(c, 1, tt, banks[8 + tt], 256, 512)
+                o_store(c, 1, 0, 4, 256, 512)
                 o_quant(c, 0)
-                o_inter(c, 1, 256, 352, False)
-                o_inter(c, 1, 352, 512, True)
+                o_inter(c, 1, 256, 384, False)
+                o_inter(c, 1, 384, 512, True)
                 o_quant(c, 1, 0, 256)
                 o_quant(c, 1, 256, 512)
                 scale_store(c)

from contextlib import ExitStack

import concourse.mybir as mybir
from concourse.masks import make_identity

N, D, K = 2048, 1024, 512
FLOPS = 4 * N * D * K

F32 = mybir.dt.float32
BF16 = mybir.dt.bfloat16
U32 = mybir.dt.uint32
I32 = mybir.dt.int32
U8 = mybir.dt.uint8
FP8X4 = mybir.dt.float8_e4m3fn_x4
ALU = mybir.AluOpType
ACT = mybir.ActivationFunctionType

P = 128
CH = 512
NCH = N // CH
NH = D // 512


def tile_ordinaldepththresholdfeaturegradient_x1_kernel(tc, x, g, w, s, b, y, t, out_0, out_1, out_2):
    nc = tc.nc
    with ExitStack() as ctx:
        keep = ctx.enter_context(tc.tile_pool(name="keep", bufs=1))
        xin = ctx.enter_context(tc.tile_pool(name="xin", bufs=NCH))
        work = ctx.enter_context(tc.tile_pool(name="work", bufs=2))
        outs = ctx.enter_context(tc.tile_pool(name="outs", bufs=4))
        psum = ctx.enter_context(tc.psum_pool(name="psum", bufs=2))
        psum_o = ctx.enter_context(tc.psum_pool(name="psum_o", bufs=4))
        ctx.enter_context(tc.manual_schedule())

        w_raw = keep.tile([P, NH, 4, K], BF16, align_bytes=64, name="w_raw")
        w_v = w.rearrange("(h p j) k -> p h j k", h=NH, j=4)
        x_raw = []
        for c in range(NCH):
            if c == 1:
                for h in range(NH):
                    nc.sync.dma_start(out=w_raw[:, h], in_=w_v[:, h])
            xr = xin.tile([P, 4, D], BF16, align_bytes=64, name="xr")
            xv = x[c * CH : (c + 1) * CH, :].rearrange("(p t) d -> p t d", t=4)
            for tp in range(2):
                nc.sync.dma_start(out=xr[:, 2 * tp : 2 * tp + 2, :], in_=xv[:, 2 * tp : 2 * tp + 2, :])
            x_raw.append(xr)
        cols = keep.tile([P, 8, 16], BF16, align_bytes=64, name="cols")
        nc.scalar.dma_start(out=cols[:, 0, 0:8].rearrange("p (h i) -> p h i", h=NH), in_=g.rearrange("(h p i) -> p h i", h=NH, i=4))
        nc.scalar.dma_start(out=cols[:, 1, :].rearrange("p (c i) -> p c i", c=NCH), in_=y.rearrange("(c p i) -> p c i", c=NCH, i=4))
        for i, v in enumerate((t, s, b)):
            nc.scalar.dma_start(out=cols[:, 2 + i, 0:4], in_=v.rearrange("(p i) -> p i", i=4))

        warm = keep.tile([P, 1], F32, name="warm")
        warm2 = keep.tile([P, 1], F32, name="warm2")
        nc.vector.memset(warm[:], 0.0)
        nc.scalar.activation(out=warm2[:], in_=warm[:], func=ACT.Sigmoid)

        id32 = keep.tile([P, P], F32, align_bytes=64, name="id32")
        make_identity(nc, id32[:])
        id16 = keep.tile([P, P], BF16, align_bytes=64, name="id16")
        nc.vector.tensor_copy(out=id16[:], in_=id32[:])
        vec32 = keep.tile([P, 3, 4], F32, align_bytes=64, name="vec32")
        nc.vector.tensor_copy(out=vec32[:], in_=cols[:, 2:5, 0:4])
        g4 = cols[:, 0, 0:8].rearrange("p (h u e) -> p h u e", h=NH, u=2)

        y_bc = keep.tile([P, N], BF16, align_bytes=64, name="y_bc")
        def y_spread(halves):
            for hf in halves:
                yp = psum_o.tile([P, N // 2], BF16, name="o_ps")
                for i in range(8):
                    j = hf * 8 + i
                    nc.tensor.transpose(
                        yp[:, i * P : (i + 1) * P],
                        cols[:, 1, j : j + 1].to_broadcast([P, P]),
                        id16[:],
                    )
                nc.scalar.copy(out=y_bc[:, hf * N // 2 : (hf + 1) * N // 2], in_=yp[:])

        w_gr = keep.tile([P, NH, K, 4], BF16, align_bytes=64, name="w_gr")
        w_codes = keep.tile([P, NH, K], U32, align_bytes=64, name="w_codes")
        w_scales = keep.tile([P, NH, K], U8, align_bytes=64, name="w_scales")

        def w_inter(h, eng):
            dst = w_gr[:, h].rearrange("p (q m) j -> p q m j", q=4)
            srcv = w_raw[:, h].rearrange("p j (m q) -> p q m j", q=4)
            for q in range(4):
                if eng == 0:
                    nc.scalar.copy(out=dst[:, q], in_=srcv[:, q])
                else:
                    nc.vector.tensor_copy(out=dst[:, q], in_=srcv[:, q])

        def w_quant():
            nc.vector.quantize_mx(
                out=w_codes[:].rearrange("p h k -> p (h k)").bitcast(FP8X4),
                scales=w_scales[:].rearrange("p h k -> p (h k)"),
                in_=w_gr[:].rearrange("p h k j -> p (h k j)"),
            )

        xs = {}

        def x_alloc(c):
            xs[c] = (
                work.tile([P, NH, CH, 4], BF16, align_bytes=64, name="x_gr"),
                work.tile([P, NH, CH], U32, align_bytes=64, name="x_codes"),
                work.tile([P, NH, CH], U8, align_bytes=64, name="x_scales"),
            )

        def x_turn(c, tp):
            words = x_raw[c][:].bitcast(F32)
            xts = []
            for h in range(NH):
                xt = psum.tile([P, 2, 256], F32, name="xt")
                for tt in range(2):
                    for u in range(2):
                        cols_tt = slice(tt * P, (tt + 1) * P)
                        nc.tensor.transpose(
                            xt[:, u, cols_tt],
                            words[:, 2 * tp + tt, 256 * h + u : 256 * (h + 1) : 2],
                            id32[:],
                        )
                xts.append(xt)
            return xts

        def x_mul(c, tp, xts):
            for h in range(NH):
                nc.vector.tensor_tensor(
                    out=xs[c][0][:, h, 256 * tp : 256 * (tp + 1), :].rearrange("p n (u e) -> p n u e", u=2),
                    in0=xts[h][:].bitcast(BF16).rearrange("p u (n e) -> p n u e", e=2),
                    in1=g4[:, h].unsqueeze(1).to_broadcast([P, 256, 2, 2]),
                    op=ALU.mult,
                )

        def x_quant(c):
            gr, codes, scales = xs[c]
            nc.vector.quantize_mx(
                out=codes[:].rearrange("p h n -> p (h n)").bitcast(FP8X4),
                scales=scales[:].rearrange("p h n -> p (h n)"),
                in_=gr[:].rearrange("p h n j -> p (h n j)"),
            )

        wt_gr = keep.tile([P, D, 4], BF16, align_bytes=64, name="wt_gr")
        wt_codes = keep.tile([P, D], U32, align_bytes=64, name="wt_codes")
        wt_scales = keep.tile([P, D], U8, align_bytes=64, name="wt_scales")

        def wt_turn(blocks):
            words = w_raw[:].bitcast(F32)
            dst = wt_gr[:].rearrange("p d e -> p (d e)").bitcast(F32).rearrange("p (h m j u) -> p h m j u", h=NH, j=4, u=2)
            for blk in blocks:
                h, jp = blk // 2, blk % 2
                wt = psum_o.tile([P, 2, 2, P], F32, name="o_ps")
                for jj in range(2):
                    for u in range(2):
                        nc.tensor.transpose(wt[:, jj, u, :], words[:, h, 2 * jp + jj, u : 256 : 2], id32[:])
                nc.scalar.copy(out=dst[:, h, :, 2 * jp : 2 * jp + 2, :], in_=wt[:].rearrange("p j u m -> p m j u"))

        def wt_quant():
            nc.vector.quantize_mx(
                out=wt_codes[:].bitcast(FP8X4), scales=wt_scales[:], in_=wt_gr[:].rearrange("p d j -> p (d j)")
            )

        g_bc = keep.tile([P, D], BF16, align_bytes=64, name="g_bc")

        def g_spread():
            gp = psum_o.tile([P, 4, P], F32, name="o_ps")
            gw = cols[:, 0, :].bitcast(F32)
            for i in range(4):
                nc.tensor.transpose(gp[:, i, :], gw[:, i : i + 1].to_broadcast([P, P]), id32[:])
            nc.scalar.copy(
                out=g_bc[:].bitcast(F32).rearrange("p (h m u) -> p h m u", h=NH, u=2),
                in_=gp[:].rearrange("p (h u) m -> p h m u", h=NH),
            )

        ls = keep.tile([P, 4, N], BF16, align_bytes=64, name="ls")

        def labels(q):
            nc.vector.tensor_scalar(
                out=ls[:, q, :],
                in0=y_bc[:],
                scalar1=vec32[:, 0, q : q + 1],
                scalar2=vec32[:, 1, q : q + 1],
                op0=ALU.is_gt,
                op1=ALU.mult,
            )

        ds = {}

        def d_alloc(c):
            ds[c] = dict(
                sig=work.tile([P, 4, CH], F32, align_bytes=64, name="sig"),
                d=work.tile([P, 4, CH], F32, align_bytes=64, name="d32"),
                gr=work.tile([P, CH, 4], BF16, align_bytes=64, name="d_gr"),
                codes=work.tile([P, CH], U32, align_bytes=64, name="d_codes"),
                scales=work.tile([P, CH], U8, align_bytes=64, name="d_scales"),
            )

        def mm1(c, q):
            z = psum.tile([P, CH], F32, name="z")
            for h in range(NH):
                nc.tensor.matmul_mx(
                    out=z[:],
                    lhsT=w_codes[:, h, q * P : (q + 1) * P].bitcast(FP8X4),
                    lhsT_scale=w_scales[:, h, q * P : (q + 1) * P],
                    rhs=xs[c][1][:, h].bitcast(FP8X4),
                    rhs_scale=xs[c][2][:, h],
                    start=(h == 0),
                    stop=(h == NH - 1),
                )
            nc.scalar.activation(
                out=ds[c]["sig"][:, q, :],
                in_=z[:],
                func=ACT.Sigmoid,
                bias=vec32[:, 2, q : q + 1],
                scale=vec32[:, 1, q : q + 1],
            )

        def d_sub(c, q):
            nc.vector.scalar_tensor_tensor(
                out=ds[c]["d"][:, q, :],
                in0=ds[c]["sig"][:, q, :],
                scalar=vec32[:, 1, q : q + 1],
                in1=ls[:, q, c * CH : (c + 1) * CH],
                op0=ALU.mult,
                op1=ALU.subtract,
            )

        def inter(dst, srct, lo, hi, on_vector):
            o = dst[:, lo:hi, :].rearrange("p (c i) q -> p c q i", i=4)
            i_ = srct[:, :, lo:hi].rearrange("p q (c i) -> p c q i", i=4)
            if on_vector:
                nc.vector.tensor_copy(out=o, in_=i_)
            else:
                nc.scalar.copy(out=o, in_=i_)

        def d_quant(c):
            e = ds[c]
            nc.vector.quantize_mx(
                out=e["codes"][:].bitcast(FP8X4), scales=e["scales"][:], in_=e["gr"][:].rearrange("p n j -> p (n j)")
            )

        outp = {}

        def o_alloc(c, dh):
            outp[(c, dh)] = dict(
                o=outs.tile([P, 4, 512], F32, align_bytes=64, name="o32"),
                gr=outs.tile([P, 512, 4], BF16, align_bytes=64, name="o_gr"),
                codes=outs.tile([P, 512], U32, align_bytes=64, name="o_codes"),
            )
            if dh == 0:
                outp[c] = work.tile([P, D], U8, align_bytes=64, name="o_scales")

        def mm2(c, dh, tt, lo=0, hi=512):
            o = psum_o.tile([P, hi - lo], F32, name="o_ps")
            nc.tensor.matmul_mx(
                out=o[:],
                lhsT=ds[c]["codes"][:, tt * P : (tt + 1) * P].bitcast(FP8X4),
                lhsT_scale=ds[c]["scales"][:, tt * P : (tt + 1) * P],
                rhs=wt_codes[:, dh * 512 + lo : dh * 512 + hi].bitcast(FP8X4),
                rhs_scale=wt_scales[:, dh * 512 + lo : dh * 512 + hi],
                start=True,
                stop=True,
            )
            return o

        def o_mul(c, dh, tt, o, lo=0, hi=512):
            nc.vector.tensor_tensor(
                out=outp[(c, dh)]["o"][:, tt, lo:hi], in0=o[:], in1=g_bc[:, dh * 512 + lo : dh * 512 + hi], op=ALU.mult
            )

        def o_store(c, dh, t0, t1, lo=0, hi=512):
            nc.sync.dma_start(
                out=out_0[c * CH : (c + 1) * CH, dh * 512 + lo : dh * 512 + hi].rearrange("(p t) d -> p t d", t=4)[:, t0:t1, :],
                in_=outp[(c, dh)]["o"][:, t0:t1, lo:hi],
            )

        def o_quant(c, dh, lo=0, hi=512):
            e = outp[(c, dh)]
            nc.vector.quantize_mx(
                out=e["codes"][:, lo:hi].bitcast(FP8X4),
                scales=outp[c][:, dh * 512 + lo : dh * 512 + hi],
                in_=e["gr"][:, lo:hi, :].rearrange("p d j -> p (d j)"),
            )
            nc.sync.dma_start(
                out=out_1[c, :, dh * 512 + lo : dh * 512 + hi, :].rearrange("p m t -> p (m t)").bitcast(I32),
                in_=e["codes"][:, lo:hi].bitcast(I32),
            )

        def scale_store(c):
            for qd in range(4):
                nc.sync.dma_start(
                    out=out_2[c, 4 * qd : 4 * qd + 4, :].bitcast(I32),
                    in_=outp[c][32 * qd : 32 * qd + 4, :].bitcast(I32),
                )

        def o_inter(c, dh, lo, hi, on_vector):
            inter(outp[(c, dh)]["gr"], outp[(c, dh)]["o"], lo, hi, on_vector)

        def d_inter(c, lo, hi, on_vector):
            inter(ds[c]["gr"], ds[c]["d"], lo, hi, on_vector)

        d_split = [0,0,0,0]

        def d_turn(c):
            if d_split[c] > 0:
                d_inter(c, 0, d_split[c], True)
            d_inter(c, d_split[c], CH, False)

        x_alloc(0)
        x_mul(0, 0, x_turn(0, 0))
        x_mul(0, 1, x_turn(0, 1))
        w_inter(0, 0)
        y_spread((0, 1))
        w_inter(1, 0)
        x_quant(0)
        x_alloc(1)
        x_mul(1, 0, x_turn(1, 0))
        x_mul(1, 1, x_turn(1, 1))
        for q in range(4):
            labels(q)
        wt_turn((0, 1, 2, 3))
        xt20 = x_turn(2, 0)
        w_quant()
        d_alloc(0)
        mm1(0, 0)
        mm1(0, 1)
        x_quant(1)
        x_alloc(2)
        x_mul(2, 0, xt20)
        xt21 = x_turn(2, 1)
        mm1(0, 2)
        mm1(0, 3)
        wt_quant()
        d_sub(0, 0)
        d_sub(0, 1)
        x_mul(2, 1, xt21)
        d_alloc(1)
        mm1(1, 0)
        xt30 = x_turn(3, 0)
        d_sub(0, 2)
        d_sub(0, 3)
        d_turn(0)
        x_alloc(3)
        x_mul(3, 0, xt30)
        mm1(1, 1)
        xt31 = x_turn(3, 1)
        mm1(1, 2)
        g_spread()
        mm1(1, 3)
        x_quant(2)
        d_sub(1, 0)
        d_quant(0)
        d_sub(1, 1)
        d_sub(1, 2)
        d_sub(1, 3)
        for c in range(NCH):
            last = c == NCH - 1
            ahead = c + 2 < NCH
            o_alloc(c, 0)
            o_alloc(c, 1)
            banks = [mm2(c, 0, tt) for tt in range(4)]
            if not last:
                if ahead:
                    d_alloc(c + 2)
                o_mul(c, 0, 0, banks[0])
                banks.append(mm2(c, 1, 0))
                d_turn(c + 1)
                if ahead:
                    mm1(c + 2, 0)
                    mm1(c + 2, 1)
                for tt in range(1, 4):
                    o_mul(c, 0, tt, banks[tt])
                    banks.append(mm2(c, 1, tt))
                    if tt % 2 == 1:
                        o_store(c, 0, tt - 1, tt + 1)
                if ahead:
                    mm1(c + 2, 2)
                    mm1(c + 2, 3)
                o_inter(c, 0, 0, 512, False)
                o_mul(c, 1, 0, banks[4])
                if c > 0:
                    o_quant(c - 1, 0)
                o_mul(c, 1, 1, banks[5])
                o_store(c, 1, 0, 2)
                if ahead:
                    d_sub(c + 2, 0)
                if c == 0:
                    x_mul(3, 1, xt31)
                o_mul(c, 1, 2, banks[6])
                d_quant(c + 1)
                o_mul(c, 1, 3, banks[7])
                o_store(c, 1, 2, 4)
                o_inter(c, 1, 0, 512, False)
                if ahead:
                    d_sub(c + 2, 1)
                if c == 0:
                    x_quant(3)
                if ahead:
                    d_sub(c + 2, 2)
                    d_sub(c + 2, 3)
                if c > 0:
                    o_quant(c - 1, 1)
                    scale_store(c - 1)
            else:
                for tt in range(4):
                    o_mul(c, 0, tt, banks[tt])
                    if tt % 2 == 1:
                        o_store(c, 0, tt - 1, tt + 1)
                    banks.append(mm2(c, 1, tt, 0, 256))
                o_quant(c - 1, 0)
                o_inter(c, 0, 0, 512, False)
                for tt in range(4):
                    o_mul(c, 1, tt, banks[4 + tt], 0, 256)
                    banks.append(mm2(c, 1, tt, 256, 512))
                o_store(c, 1, 0, 4, 0, 256)
                o_quant(c - 1, 1)
                scale_store(c - 1)
                o_inter(c, 1, 0, 256, False)
                for tt in range(4):
                    o_mul(c, 1, tt, banks[8 + tt], 256, 512)
                o_store(c, 1, 0, 4, 256, 512)
                o_quant(c, 0)
                o_inter(c, 1, 256, 384, False)
                o_inter(c, 1, 384, 512, True)
                o_quant(c, 1, 0, 256)
                o_quant(c, 1, 256, 512)
                scale_store(c)
